import numpy as np
import ml_dtypes


def mxq(x, axis, fmt="e4m3"):
    dtype, down = {"e4m3": (ml_dtypes.float8_e4m3fn, 7), "e5m2": (ml_dtypes.float8_e5m2, 14)}[fmt]
    v = np.moveaxis(np.asarray(x, np.float32).astype(ml_dtypes.bfloat16).astype(np.float64), axis, -1)
    blocks = v.reshape(v.shape[:-1] + (-1, 32))
    amax = np.abs(blocks).max(-1, keepdims=True)
    byte = np.maximum(np.where(amax > 0, np.frexp(amax)[1] - 1 + 127, 0) - down, 1)
    scale = np.exp2(byte - 127.0)
    codes = (blocks / scale).astype(np.float32).astype(dtype).astype(np.float64)
    return np.moveaxis((codes * scale).reshape(v.shape), -1, axis)


WIDE = False


def mx_kscale(k):
    if not WIDE:
        return np.ones(k)
    levels = np.array([10, -10, 5, -5, 0])
    if k % 512:
        return np.exp2(np.random.permutation(np.resize(levels, k // 32))).repeat(32)
    a = np.empty((k // 512, 16))
    for p in range(k // 512):
        a[p, :8] = np.random.permutation(np.resize(levels, 8))
        for g in range(8):
            far = levels[np.abs(levels - a[p, g]) >= 10]
            a[p, g + 8] = far[np.random.randint(len(far))]
    return np.exp2(a.ravel()).repeat(32)


def f64(x):
    return np.asarray(x).astype(np.float64)


def striped(idx):
    return np.tile(idx.reshape(-1, 16).T, (8, 1)).astype(np.uint16)


def unstriped(offs):
    return offs[:16].T.reshape(-1).astype(np.int64)


def striped8(idx):
    return np.concatenate([x.reshape(-1, 16).T for x in idx]).astype(np.uint16)


def runs(offs, k):
    lists = np.stack([offs[16 * r : 16 * r + 16].T.reshape(-1) for r in range(8)]).astype(np.int64)
    return lists[np.arange(k) % 512 // 64]


def pack_weight(w):
    k, n = w.shape
    w = f64(np.asarray(w, np.float32).astype(ml_dtypes.bfloat16)).reshape(k // 32, 32, n)
    amax = np.abs(w).max(1)
    byte = np.clip(np.where(amax > 0, np.frexp(amax)[1] - 1 + 127 - 7, 1), 1, 254)
    scaled = (w * np.exp2(127.0 - byte)[:, None, :]).reshape(k, n).astype(np.float32)
    words = np.ascontiguousarray(scaled.reshape(k // 512, 128, 4, n).transpose(0, 1, 3, 2)).astype(ml_dtypes.float8_e4m3fn).view(np.uint8)
    return words, np.ascontiguousarray(byte.astype(np.uint8).reshape(k // 512, 16, n))


def unpack_weight(words, scales):
    g, p, n, _ = words.shape
    vals = np.ascontiguousarray(words).view(ml_dtypes.float8_e4m3fn).astype(np.float64) * np.repeat(np.exp2(scales.astype(np.float64) - 127.0), 8, axis=1)[..., None]
    return vals.transpose(0, 1, 3, 2).reshape(g * 512, n)


def sigmoid(v):
    return 1.0 / (1.0 + np.exp(-np.maximum(v, -700.0)))

def planes(y):
    n, m = y.shape
    v = y.astype(np.float32).astype(ml_dtypes.bfloat16).astype(np.float64).reshape(n // 32, 32, m)
    top = np.abs(v).max(1)
    byte = np.clip(np.where(top > 0, np.frexp(top)[1] - 1 + 127 - 7, 1), 1, 254)
    codes = (v * np.exp2(127.0 - byte)[:, None, :]).reshape(n, m).astype(np.float32).astype(ml_dtypes.float8_e4m3fn).view(np.uint8)
    words = codes.reshape(n // 512, 128, 4, m).transpose(0, 1, 3, 2)
    return np.ascontiguousarray(words), np.ascontiguousarray(byte.astype(np.uint8).reshape(n // 512, 16, m))


K, T, S, N, G, H = 512, 2048, 512, 512, 2048, 512


def setup_inputs():
    n = np.random.standard_normal
    s = mx_kscale(K)[:, None]
    u = mx_kscale(S)
    packed_xT = pack_weight(n((K, T)) * s)
    packed_dT = pack_weight(n((K, G)) / s)
    packed_w1 = pack_weight(n((H, N)) / np.sqrt(H) / u[:, None])
    return {
        "x_words": packed_xT[0],
        "x_scales": packed_xT[1],
        "d_words": packed_dT[0],
        "d_scales": packed_dT[1],
        "sl": np.random.uniform(1.0, 2.0, (H, 1)).astype(np.float32),
        "th": (0.5 * n((H, 1))).astype(np.float32),
        "gn": (np.random.uniform(0.5, 1.5, (H, 1)) * u[:, None]).astype(np.float32),
        "w1_words": packed_w1[0],
        "w1_scales": packed_w1[1],
        "sl2": np.random.uniform(1.0, 2.0, (N, 1)).astype(np.float32),
        "th2": (0.5 * n((N, 1))).astype(np.float32),
        "offs": striped8(np.random.randint(0, T, (8, S))),
        "k1": striped8(np.random.randint(0, G, (8, H))),
        "n1": striped(np.random.permutation(S)),
        "n2": striped(np.random.permutation(S)),
        "n3": striped8(np.stack([np.random.permutation(S) for _ in range(8)])),
        "n4": striped8(np.stack([np.random.permutation(S) for _ in range(8)])),
    }


def reference(x_words, x_scales, d_words, d_scales, sl, th, gn, w1_words, w1_scales, sl2, th2, offs, k1, n1, n2, n3, n4):
    d_k1 = unpack_weight(d_words, d_scales)[np.arange(K)[:, None], runs(k1, K)]
    xq = unpack_weight(x_words, x_scales)[np.arange(K)[:, None], runs(offs, K)]
    h = 0.0625 * (d_k1.T @ xq)
    pa = h[:, unstriped(n1)]
    sg = sigmoid(f64(sl) * (h[:, unstriped(n2)] - f64(th)))
    z = f64(gn) * (pa + sg * (h - pa))
    h2 = unpack_weight(w1_words, w1_scales).T @ mxq(z, 0, "e4m3")
    st = h2 - (h2[np.arange(N)[:, None], runs(n3, N)])
    sg2 = sigmoid(f64(sl2) * (st[np.arange(N)[:, None], runs(n4, N)] - f64(th2)))
    out_0 = h2 * sg2
    return (out_0,) + planes(out_0)

@@ -1,0 +1,221 @@
+from contextlib import ExitStack
+
+import concourse.mybir as mybir
+
+F32 = mybir.dt.float32
+BF16 = mybir.dt.bfloat16
+I32 = mybir.dt.int32
+U32 = mybir.dt.uint32
+U16 = mybir.dt.uint16
+U8 = mybir.dt.uint8
+FP8X4 = mybir.dt.float8_e4m3fn_x4
+ACT = mybir.ActivationFunctionType
+ALU = mybir.AluOpType
+
+P = 128
+PACK = 4
+S = 512
+TABLE = 2048
+HALF = S // 2
+LIST_COLS = S // 16
+FLOPS = 2 * 2 * 512 * 512 * 512
+
+
+def tile_picked_hpqeblehq_none_po_kernel(
+    tc, x_words, x_scales, d_words, d_scales, sl, th, gn, w1_words, w1_scales, sl2, th2,
+    offs, k1, n1, n2, n3, n4, out_0, out_1, out_2,
+):
+    nc = tc.nc
+    with ExitStack() as ctx:
+        sb = ctx.enter_context(tc.tile_pool(name="sb", bufs=1))
+        ps = ctx.enter_context(tc.psum_pool(name="ps", bufs=1))
+
+        def tile(name, shape, dtype):
+            return sb.tile(shape, dtype, name=name, align_bytes=64)
+
+        def load_list(name, src):
+            dst = tile(name, [P, LIST_COLS], U16)
+            nc.sync.dma_start(dst[:], src)
+            return dst
+
+        def load_words(name, src, width, queue):
+            dst = tile(name, [P, width], U32)
+            queue.dma_start(dst[:].bitcast(I32), src[0].rearrange("p n t -> p (n t)").bitcast(I32))
+            return dst
+
+        def load_rows(name, src):
+            dst = tile(name, [P, PACK], F32)
+            nc.gpsimd.dma_start(dst[:], src.rearrange("(p t) o -> p (t o)", t=PACK))
+            return dst
+
+        def cols(half):
+            return slice(half * HALF, (half + 1) * HALF)
+
+        def entries(lst, half):
+            return lst[:, half * LIST_COLS // 2 : (half + 1) * LIST_COLS // 2]
+
+        def deal_words(t):
+            return t[:].rearrange("p (t c i) -> p c t i", t=PACK, i=4)
+
+        def undealt_words(t):
+            return t[:].rearrange("p (c i t) -> p c t i", t=PACK, i=4)
+
+        def woven(t):
+            return t[:].rearrange("p (c i) t -> p c t i", i=2)
+
+        def planar(t):
+            return t[:].rearrange("p t (c i) -> p c t i", i=2)
+
+        d_bytes = tile("d_bytes", [P, TABLE], U8)
+        x_bytes = tile("x_bytes", [P, TABLE], U8)
+        w_bytes = tile("w_bytes", [P, S], U8)
+        planes = tile("planes", [P, 3 * S], U8)
+        nc.vector.memset(d_bytes[:].bitcast(I32), 0)
+        nc.vector.memset(x_bytes[:].bitcast(I32), 0)
+        nc.vector.memset(w_bytes[:].bitcast(I32), 0)
+        nc.vector.memset(planes[:].bitcast(I32), 0)
+        k1_t = load_list("k1_t", k1)
+        offs_t = load_list("offs_t", offs)
+        d_tab = load_words("d_tab", d_words, TABLE, nc.sync)
+        x_tab = load_words("x_tab", x_words, TABLE, nc.sync)
+        nc.scalar.dma_start(d_bytes[0:P:8, :].bitcast(I32), d_scales[0].bitcast(I32))
+        nc.scalar.dma_start(x_bytes[0:P:8, :].bitcast(I32), x_scales[0].bitcast(I32))
+        nc.scalar.dma_start(w_bytes[0:P:8, :].bitcast(I32), w1_scales[0].bitcast(I32))
+        n2_t = load_list("n2_t", n2)
+        n1_t = load_list("n1_t", n1)
+        w_raw = load_words("w_raw", w1_words, S, nc.sync)
+        n3_t = load_list("n3_t", n3)
+        n4_t = load_list("n4_t", n4)
+
+        staged = tile("staged", [P, 3 * S], U8)
+        sl_t = load_rows("sl_t", sl)
+        th_t = load_rows("th_t", th)
+        gn_t = load_rows("gn_t", gn)
+        sl2_t = load_rows("sl2_t", sl2)
+        th2_t = load_rows("th2_t", th2)
+
+        def negated(name, src):
+            dst = tile(name, [P, PACK], F32)
+            nc.gpsimd.tensor_scalar(dst[:], src[:], -1.0, 0.0, ALU.mult, ALU.add)
+            return dst
+
+        def sigmoid_bias(name, slope, threshold):
+            dst = tile(name, [P, PACK], F32)
+            nc.gpsimd.tensor_tensor(dst[:], negated(name + "_neg", slope)[:], threshold[:], ALU.mult)
+            return dst
+
+        bias1 = sigmoid_bias("bias1", sl_t, th_t)
+        neg_gn = negated("neg_gn", gn_t)
+        bias2 = sigmoid_bias("bias2", sl2_t, th2_t)
+
+        def deal_bytes(engine, dst, src):
+            engine.tensor_copy(dst.rearrange("p (t m) -> p t m", t=PACK), src.rearrange("p (m t) -> p t m", t=PACK))
+
+        d_bytes_g = tile("d_bytes_g", [P, S], U8)
+        x_bytes_g = tile("x_bytes_g", [P, S], U8)
+        deal_bytes(nc.gpsimd, staged[:, 2 * S : 3 * S], w_bytes[:])
+        nc.vector.tensor_copy(d_bytes_g[:], d_bytes[:].indirect(k1_t[:]))
+        nc.vector.tensor_copy(x_bytes_g[:], x_bytes[:].indirect(offs_t[:]))
+        deal_bytes(nc.vector, staged[:, 0:S], d_bytes_g[:])
+        nc.vector.tensor_copy(staged[:, S : 2 * S].bitcast(I32), x_bytes_g[:].bitcast(I32))
+        for j in range(4):
+            nc.scalar.dma_start(planes[j:P:32, :].bitcast(I32), staged[8 * j : P : 32, :].bitcast(I32))
+
+        d_g = tile("d_g", [P, S], U32)
+        d_dealt = tile("d_dealt", [P, S], U32)
+        nc.vector.tensor_copy(d_g[:], d_tab[:].indirect(k1_t[:]))
+        nc.vector.tensor_copy(deal_words(d_dealt).bitcast(I32), undealt_words(d_g).bitcast(I32))
+
+        w_dealt = tile("w_dealt", [P, S], U32)
+        nc.gpsimd.tensor_copy(w_dealt[:].rearrange("p (t m) -> p t m", t=PACK), w_raw[:].rearrange("p (m t) -> p t m", t=PACK))
+
+        banks = [[ps.tile([P, HALF], F32, name="bank%d%d" % (t, hf)) for hf in range(2)] for t in range(PACK)]
+        h = [tile("h%d" % t, [P, S], F32) for t in range(PACK)]
+        x_g = [tile("x_g%d" % hf, [P, HALF], U32) for hf in range(2)]
+        for hf in range(2):
+            nc.vector.tensor_copy(x_g[hf][:], x_tab[:].indirect(entries(offs_t, hf)))
+
+        def h_bank(t, hf):
+            return banks[t][hf] if t < 3 else banks[hf][1]
+
+        def multiply_h(t, hf):
+            m = slice(t * P, (t + 1) * P)
+            nc.tensor.matmul_mx(
+                out=h_bank(t, hf)[:], lhsT=d_dealt[:, m].bitcast(FP8X4), lhsT_scale=planes[:, m],
+                rhs=x_g[hf][:].bitcast(FP8X4), rhs_scale=planes[:, S + hf * HALF : S + (hf + 1) * HALF],
+                start=True, stop=True,
+            )
+
+        def empty_h(t, hf, on_scalar):
+            if on_scalar:
+                nc.scalar.activation(h[t][:, cols(hf)], h_bank(t, hf)[:], ACT.Copy, scale=0.0625)
+            else:
+                nc.vector.tensor_scalar_mul(h[t][:, cols(hf)], h_bank(t, hf)[:], 0.0625)
+
+        for t, hf in ((0, 0), (1, 0), (0, 1), (1, 1), (2, 0), (2, 1)):
+            multiply_h(t, hf)
+            empty_h(t, hf, False)
+
+        h2 = [tile("h2_%d" % t, [P, S], F32) for t in range(PACK)]
+        neg_h2 = [tile("neg_h2_%d" % t, [P, S], F32) for t in range(PACK)]
+        for hf in range(2):
+            kept = tile("kept%d" % hf, [P, PACK, HALF], F32)
+            mixed = tile("mixed%d" % hf, [P, PACK, HALF], F32)
+            for t in range(PACK):
+                if hf == 0 and t == 2:
+                    for part in range(2):
+                        multiply_h(3, part)
+                        empty_h(3, part, True)
+                sg = tile("sg%d%d" % (t, hf), [P, HALF], F32)
+                rest = tile("rest%d%d" % (t, hf), [P, HALF], F32)
+                nc.scalar.activation(
+                    sg[:], h[t][:].indirect(entries(n2_t, hf)), ACT.Sigmoid,
+                    bias=bias1[:, t : t + 1], scale=sl_t[:, t : t + 1],
+                )
+                nc.scalar.activation(rest[:], sg[:], ACT.Identity, bias=gn_t[:, t : t + 1], scale=neg_gn[:, t : t + 1])
+                nc.vector.scalar_tensor_tensor(kept[:, t, :], sg[:], gn_t[:, t : t + 1], h[t][:, cols(hf)], ALU.mult, ALU.mult)
+                nc.vector.tensor_tensor(mixed[:, t, :], h[t][:].indirect(entries(n1_t, hf)), rest[:], ALU.mult)
+            z = tile("z%d" % hf, [P, HALF, PACK], BF16)
+            z_words = tile("z_words%d" % hf, [P, HALF], U32)
+            z_plane = tile("z_plane%d" % hf, [P, HALF], U8)
+            nc.vector.tensor_tensor(woven(z), planar(kept), planar(mixed), ALU.add)
+            nc.vector.quantize_mx(out=z_words[:].bitcast(FP8X4), scales=z_plane[:], in_=z[:].rearrange("p c t -> p (c t)"))
+            for t in range(PACK):
+                m = slice(t * P, (t + 1) * P)
+                nc.tensor.matmul_mx(
+                    out=banks[t][hf][:], lhsT=w_dealt[:, m].bitcast(FP8X4), lhsT_scale=planes[:, 2 * S + t * P : 2 * S + (t + 1) * P],
+                    rhs=z_words[:].bitcast(FP8X4), rhs_scale=z_plane[:], start=True, stop=True,
+                )
+            for t in range(PACK):
+                if hf == 1 and t == 0:
+                    nc.vector.tensor_scalar_mul(neg_h2[t][:, cols(hf)], banks[t][hf][:], -1.0)
+                else:
+                    nc.scalar.activation(neg_h2[t][:, cols(hf)], banks[t][hf][:], ACT.Copy, scale=-1.0)
+                nc.scalar.copy(h2[t][:, cols(hf)], banks[t][hf][:])
+
+        y = [tile("y%d" % hf, [P, PACK, HALF], F32) for hf in range(2)]
+        out_rows = out_0.rearrange("(p t) j -> p t j", t=PACK)
+        st = [tile("st%d" % t, [P, S], F32) for t in range(PACK)]
+        for t in range(PACK):
+            for hf in range(2):
+                nc.vector.tensor_tensor(st[t][:, cols(hf)], neg_h2[t][:].indirect(entries(n3_t, hf)), h2[t][:, cols(hf)], ALU.add)
+        y_plane = tile("y_plane", [P, S], U8)
+        words_out = out_1[0].rearrange("p n t -> p (n t)").bitcast(I32)
+        for t in range(PACK):
+            for hf in range(2):
+                sg2 = tile("sg2_%d%d" % (t, hf), [P, HALF], F32)
+                nc.scalar.activation(
+                    sg2[:], st[t][:].indirect(entries(n4_t, hf)), ACT.Sigmoid,
+                    bias=bias2[:, t : t + 1], scale=sl2_t[:, t : t + 1],
+                )
+                nc.vector.tensor_tensor(y[hf][:, t, :], h2[t][:, cols(hf)], sg2[:], ALU.mult)
+                nc.sync.dma_start(out_rows[:, t, cols(hf)], y[hf][:, t, :])
+        for hf in range(2):
+            y_bf = tile("y_bf%d" % hf, [P, HALF, PACK], BF16)
+            y_words = tile("y_words%d" % hf, [P, HALF], U32)
+            nc.vector.tensor_copy(woven(y_bf), planar(y[hf]))
+            nc.vector.quantize_mx(out=y_words[:].bitcast(FP8X4), scales=y_plane[:, cols(hf)], in_=y_bf[:].rearrange("p c t -> p (c t)"))
+            nc.sync.dma_start(words_out[:, cols(hf)], y_words[:].bitcast(I32))
+        for q in range(4):
+            queue = nc.scalar if q % 2 == 0 else nc.sync
+            queue.dma_start(out_2[0][4 * q : 4 * q + 4, :].bitcast(I32), y_plane[32 * q : 32 * q + 4, :].bitcast(I32))

@@ -43,9 +43,9 @@ def tile_picked_hpqeblehq_none_po_kernel(
             queue.dma_start(dst[:].bitcast(I32), src[0].rearrange("p n t -> p (n t)").bitcast(I32))
             return dst
 
-        def load_rows(name, src):
+        def load_rows(name, src, queue):
             dst = tile(name, [P, PACK], F32)
-            nc.gpsimd.dma_start(dst[:], src.rearrange("(p t) o -> p (t o)", t=PACK))
+            queue.dma_start(dst[:], src.rearrange("(p t) o -> p (t o)", t=PACK))
             return dst
 
         def cols(half):
@@ -76,23 +76,24 @@ def tile_picked_hpqeblehq_none_po_kernel(
         nc.vector.memset(planes[:].bitcast(I32), 0)
         k1_t = load_list("k1_t", k1)
         offs_t = load_list("offs_t", offs)
+        nc.sync.dma_start(d_bytes[0:P:8, :].bitcast(I32), d_scales[0].bitcast(I32))
+        nc.sync.dma_start(x_bytes[0:P:8, :].bitcast(I32), x_scales[0].bitcast(I32))
         d_tab = load_words("d_tab", d_words, TABLE, nc.sync)
         x_tab = load_words("x_tab", x_words, TABLE, nc.sync)
-        nc.scalar.dma_start(d_bytes[0:P:8, :].bitcast(I32), d_scales[0].bitcast(I32))
-        nc.scalar.dma_start(x_bytes[0:P:8, :].bitcast(I32), x_scales[0].bitcast(I32))
         nc.scalar.dma_start(w_bytes[0:P:8, :].bitcast(I32), w1_scales[0].bitcast(I32))
+        sl_t = load_rows("sl_t", sl, nc.scalar)
+        th_t = load_rows("th_t", th, nc.scalar)
+        gn_t = load_rows("gn_t", gn, nc.gpsimd)
         n2_t = load_list("n2_t", n2)
         n1_t = load_list("n1_t", n1)
         w_raw = load_words("w_raw", w1_words, S, nc.sync)
         n3_t = load_list("n3_t", n3)
         n4_t = load_list("n4_t", n4)
-
+        sl2_t = load_rows("sl2_t", sl2, nc.sync)
+        th2_t = load_rows("th2_t", th2, nc.sync)
         staged = tile("staged", [P, 3 * S], U8)
-        sl_t = load_rows("sl_t", sl)
-        th_t = load_rows("th_t", th)
-        gn_t = load_rows("gn_t", gn)
-        sl2_t = load_rows("sl2_t", sl2)
-        th2_t = load_rows("th2_t", th2)
+        warm = tile("warm", [P, 1], F32)
+        nc.scalar.activation(warm[:], sl_t[:, 0:1], ACT.Sigmoid)
 
         def negated(name, src):
             dst = tile(name, [P, PACK], F32)

@@ -30,8 +30,8 @@ def tile_picked_hpqeblehq_none_po_kernel(
         sb = ctx.enter_context(tc.tile_pool(name="sb", bufs=1))
         ps = ctx.enter_context(tc.psum_pool(name="ps", bufs=1))
 
-        def tile(name, shape, dtype):
-            return sb.tile(shape, dtype, name=name, align_bytes=64)
+        def tile(name, shape, dtype, tag=None):
+            return sb.tile(shape, dtype, name=name, tag=tag or name, align_bytes=64)
 
         def load_list(name, src):
             dst = tile(name, [P, LIST_COLS], U16)
@@ -51,8 +51,8 @@ def tile_picked_hpqeblehq_none_po_kernel(
         def cols(half):
             return slice(half * HALF, (half + 1) * HALF)
 
-        def entries(lst, half):
-            return lst[:, half * LIST_COLS // 2 : (half + 1) * LIST_COLS // 2]
+        def entries(lst, c):
+            return lst[:, c.start // 16 : c.stop // 16]
 
         def deal_words(t):
             return t[:].rearrange("p (t c i) -> p c t i", t=PACK, i=4)
@@ -61,37 +61,35 @@ def tile_picked_hpqeblehq_none_po_kernel(
             return t[:].rearrange("p (c i t) -> p c t i", t=PACK, i=4)
 
         def woven(t):
-            return t[:].rearrange("p (c i) t -> p c t i", i=2)
+            return t.rearrange("p (c i) t -> p c t i", i=2)
 
         def planar(t):
-            return t[:].rearrange("p t (c i) -> p c t i", i=2)
+            return t.rearrange("p t (c i) -> p c t i", i=2)
 
         d_bytes = tile("d_bytes", [P, TABLE], U8)
         x_bytes = tile("x_bytes", [P, TABLE], U8)
         w_bytes = tile("w_bytes", [P, S], U8)
         planes = tile("planes", [P, 3 * S], U8)
+        nc.vector.memset(w_bytes[:].bitcast(I32), 0)
         nc.vector.memset(d_bytes[:].bitcast(I32), 0)
         nc.vector.memset(x_bytes[:].bitcast(I32), 0)
-        nc.vector.memset(w_bytes[:].bitcast(I32), 0)
-        nc.vector.memset(planes[:].bitcast(I32), 0)
         k1_t = load_list("k1_t", k1)
         offs_t = load_list("offs_t", offs)
-        nc.sync.dma_start(d_bytes[0:P:8, :].bitcast(I32), d_scales[0].bitcast(I32))
-        nc.sync.dma_start(x_bytes[0:P:8, :].bitcast(I32), x_scales[0].bitcast(I32))
         d_tab = load_words("d_tab", d_words, TABLE, nc.sync)
-        x_tab = load_words("x_tab", x_words, TABLE, nc.sync)
-        nc.scalar.dma_start(w_bytes[0:P:8, :].bitcast(I32), w1_scales[0].bitcast(I32))
         sl_t = load_rows("sl_t", sl, nc.scalar)
         th_t = load_rows("th_t", th, nc.scalar)
+        nc.scalar.dma_start(w_bytes[0:P:8, :].bitcast(I32), w1_scales[0].bitcast(I32))
+        nc.scalar.dma_start(d_bytes[0:P:8, :].bitcast(I32), d_scales[0].bitcast(I32))
+        nc.scalar.dma_start(x_bytes[0:P:8, :].bitcast(I32), x_scales[0].bitcast(I32))
         gn_t = load_rows("gn_t", gn, nc.gpsimd)
+        sl2_t = load_rows("sl2_t", sl2, nc.gpsimd)
+        th2_t = load_rows("th2_t", th2, nc.gpsimd)
         n2_t = load_list("n2_t", n2)
         n1_t = load_list("n1_t", n1)
+        x_tab = load_words("x_tab", x_words, TABLE, nc.sync)
         w_raw = load_words("w_raw", w1_words, S, nc.sync)
         n3_t = load_list("n3_t", n3)
         n4_t = load_list("n4_t", n4)
-        sl2_t = load_rows("sl2_t", sl2, nc.sync)
-        th2_t = load_rows("th2_t", th2, nc.sync)
-        staged = tile("staged", [P, 3 * S], U8)
         warm = tile("warm", [P, 1], F32)
         nc.scalar.activation(warm[:], sl_t[:, 0:1], ACT.Sigmoid)
 
@@ -114,15 +112,15 @@ def tile_picked_hpqeblehq_none_po_kernel(
 
         d_bytes_g = tile("d_bytes_g", [P, S], U8)
         x_bytes_g = tile("x_bytes_g", [P, S], U8)
-        deal_bytes(nc.gpsimd, staged[:, 2 * S : 3 * S], w_bytes[:])
+        deal_bytes(nc.vector, planes[:, 2 * S : 3 * S], w_bytes[:])
         nc.vector.tensor_copy(d_bytes_g[:], d_bytes[:].indirect(k1_t[:]))
         nc.vector.tensor_copy(x_bytes_g[:], x_bytes[:].indirect(offs_t[:]))
-        deal_bytes(nc.vector, staged[:, 0:S], d_bytes_g[:])
-        nc.vector.tensor_copy(staged[:, S : 2 * S].bitcast(I32), x_bytes_g[:].bitcast(I32))
-        for j in range(4):
-            nc.scalar.dma_start(planes[j:P:32, :].bitcast(I32), staged[8 * j : P : 32, :].bitcast(I32))
+        deal_bytes(nc.vector, planes[:, 0:S], d_bytes_g[:])
+        nc.vector.tensor_copy(planes[:, S : 2 * S].bitcast(I32), x_bytes_g[:].bitcast(I32))
+        for q in range(4):
+            nc.scalar.dma_start(planes[32 * q + 4 : 32 * q + 8, :].bitcast(I32), planes[32 * q : 32 * q + 32 : 8, :].bitcast(I32))
 
-        d_g = tile("d_g", [P, S], U32)
+        d_g = tile("d_g", [P, S], U32, tag="x_bytes_g")
         d_dealt = tile("d_dealt", [P, S], U32)
         nc.vector.tensor_copy(d_g[:], d_tab[:].indirect(k1_t[:]))
         nc.vector.tensor_copy(deal_words(d_dealt).bitcast(I32), undealt_words(d_g).bitcast(I32))
@@ -130,11 +128,16 @@ def tile_picked_hpqeblehq_none_po_kernel(
         w_dealt = tile("w_dealt", [P, S], U32)
         nc.gpsimd.tensor_copy(w_dealt[:].rearrange("p (t m) -> p t m", t=PACK), w_raw[:].rearrange("p (m t) -> p t m", t=PACK))
 
+        h = [tile("h%d" % t, [P, S if t == 0 else 2 * S], F32) for t in range(PACK)]
+        st = [tile("st%d" % t, [P, S if t == 3 else 2 * S], F32) for t in range(PACK)]
+        for t in range(1, PACK):
+            nc.vector.memset(h[t][:, S:], 0.0)
+            nc.scalar.copy(st[t - 1][:, S:], h[t][:, S:])
+
         banks = [[ps.tile([P, HALF], F32, name="bank%d%d" % (t, hf)) for hf in range(2)] for t in range(PACK)]
-        h = [tile("h%d" % t, [P, S], F32) for t in range(PACK)]
         x_g = [tile("x_g%d" % hf, [P, HALF], U32) for hf in range(2)]
         for hf in range(2):
-            nc.vector.tensor_copy(x_g[hf][:], x_tab[:].indirect(entries(offs_t, hf)))
+            nc.vector.tensor_copy(x_g[hf][:], x_tab[:].indirect(entries(offs_t, cols(hf))))
 
         def h_bank(t, hf):
             return banks[t][hf] if t < 3 else banks[hf][1]
@@ -142,79 +145,129 @@ def tile_picked_hpqeblehq_none_po_kernel(
         def multiply_h(t, hf):
             m = slice(t * P, (t + 1) * P)
             nc.tensor.matmul_mx(
-                out=h_bank(t, hf)[:], lhsT=d_dealt[:, m].bitcast(FP8X4), lhsT_scale=planes[:, m],
-                rhs=x_g[hf][:].bitcast(FP8X4), rhs_scale=planes[:, S + hf * HALF : S + (hf + 1) * HALF],
+                out=h_bank(t, hf)[:], lhsT=d_dealt[:, m].bitcast(FP8X4), lhsT_scale=planes[4:, m],
+                rhs=x_g[hf][:].bitcast(FP8X4), rhs_scale=planes[4:, S + hf * HALF : S + (hf + 1) * HALF],
                 start=True, stop=True,
             )
 
-        def empty_h(t, hf, on_scalar):
-            if on_scalar:
+        for t, hf in ((0, 0), (1, 0), (0, 1), (1, 1), (2, 0), (2, 1)):
+            multiply_h(t, hf)
+            if hf == 0 and t < 2:
                 nc.scalar.activation(h[t][:, cols(hf)], h_bank(t, hf)[:], ACT.Copy, scale=0.0625)
             else:
                 nc.vector.tensor_scalar_mul(h[t][:, cols(hf)], h_bank(t, hf)[:], 0.0625)
 
-        for t, hf in ((0, 0), (1, 0), (0, 1), (1, 1), (2, 0), (2, 1)):
-            multiply_h(t, hf)
-            empty_h(t, hf, False)
+        def last_h(hf):
+            multiply_h(3, hf)
+            nc.scalar.activation(h[3][:, cols(hf)], h_bank(3, hf)[:], ACT.Copy, scale=0.0625)
 
+        sg = tile("sg", [P, PACK, S], F32)
+        rest = tile("rest", [P, PACK, S], F32)
+        kept = tile("kept", [P, PACK, S], F32)
+        mixed = tile("mixed", [P, PACK, S], F32)
         h2 = [tile("h2_%d" % t, [P, S], F32) for t in range(PACK)]
-        neg_h2 = [tile("neg_h2_%d" % t, [P, S], F32) for t in range(PACK)]
-        for hf in range(2):
-            kept = tile("kept%d" % hf, [P, PACK, HALF], F32)
-            mixed = tile("mixed%d" % hf, [P, PACK, HALF], F32)
-            for t in range(PACK):
-                if hf == 0 and t == 2:
-                    for part in range(2):
-                        multiply_h(3, part)
-                        empty_h(3, part, True)
-                sg = tile("sg%d%d" % (t, hf), [P, HALF], F32)
-                rest = tile("rest%d%d" % (t, hf), [P, HALF], F32)
-                nc.scalar.activation(
-                    sg[:], h[t][:].indirect(entries(n2_t, hf)), ACT.Sigmoid,
-                    bias=bias1[:, t : t + 1], scale=sl_t[:, t : t + 1],
-                )
-                nc.scalar.activation(rest[:], sg[:], ACT.Identity, bias=gn_t[:, t : t + 1], scale=neg_gn[:, t : t + 1])
-                nc.vector.scalar_tensor_tensor(kept[:, t, :], sg[:], gn_t[:, t : t + 1], h[t][:, cols(hf)], ALU.mult, ALU.mult)
-                nc.vector.tensor_tensor(mixed[:, t, :], h[t][:].indirect(entries(n1_t, hf)), rest[:], ALU.mult)
+        neg_h2 = h
+
+        def gate(t, c):
+            nc.scalar.activation(
+                sg[:, t, c], h[t][:].indirect(entries(n2_t, c)), ACT.Sigmoid,
+                bias=bias1[:, t : t + 1], scale=sl_t[:, t : t + 1],
+            )
+
+        def complement(t, c, on_scalar):
+            if on_scalar:
+                nc.scalar.activation(rest[:, t, c], sg[:, t, c], ACT.Identity, bias=gn_t[:, t : t + 1], scale=neg_gn[:, t : t + 1])
+            else:
+                nc.vector.tensor_scalar(rest[:, t, c], sg[:, t, c], neg_gn[:, t : t + 1], gn_t[:, t : t + 1], ALU.mult, ALU.add)
+
+        def keep(t, c):
+            nc.vector.scalar_tensor_tensor(kept[:, t, c], sg[:, t, c], gn_t[:, t : t + 1], h[t][:, c], ALU.mult, ALU.mult)
+
+        def mix(t, c):
+            nc.vector.tensor_tensor(mixed[:, t, c], h[t][:].indirect(entries(n1_t, c)), rest[:, t, c], ALU.mult)
+
+        def second_product(hf):
             z = tile("z%d" % hf, [P, HALF, PACK], BF16)
             z_words = tile("z_words%d" % hf, [P, HALF], U32)
             z_plane = tile("z_plane%d" % hf, [P, HALF], U8)
-            nc.vector.tensor_tensor(woven(z), planar(kept), planar(mixed), ALU.add)
+            nc.vector.tensor_tensor(woven(z[:]), planar(kept[:, :, cols(hf)]), planar(mixed[:, :, cols(hf)]), ALU.add)
             nc.vector.quantize_mx(out=z_words[:].bitcast(FP8X4), scales=z_plane[:], in_=z[:].rearrange("p c t -> p (c t)"))
             for t in range(PACK):
-                m = slice(t * P, (t + 1) * P)
                 nc.tensor.matmul_mx(
-                    out=banks[t][hf][:], lhsT=w_dealt[:, m].bitcast(FP8X4), lhsT_scale=planes[:, 2 * S + t * P : 2 * S + (t + 1) * P],
+                    out=banks[t][hf][:], lhsT=w_dealt[:, t * P : (t + 1) * P].bitcast(FP8X4),
+                    lhsT_scale=planes[4:, 2 * S + t * P : 2 * S + (t + 1) * P],
                     rhs=z_words[:].bitcast(FP8X4), rhs_scale=z_plane[:], start=True, stop=True,
                 )
-            for t in range(PACK):
-                if hf == 1 and t == 0:
-                    nc.vector.tensor_scalar_mul(neg_h2[t][:, cols(hf)], banks[t][hf][:], -1.0)
-                else:
-                    nc.scalar.activation(neg_h2[t][:, cols(hf)], banks[t][hf][:], ACT.Copy, scale=-1.0)
-                nc.scalar.copy(h2[t][:, cols(hf)], banks[t][hf][:])
 
-        y = [tile("y%d" % hf, [P, PACK, HALF], F32) for hf in range(2)]
-        out_rows = out_0.rearrange("(p t) j -> p t j", t=PACK)
-        st = [tile("st%d" % t, [P, S], F32) for t in range(PACK)]
+        def empty_h2(t, hf):
+            if hf == 1 and t == 0:
+                nc.vector.tensor_scalar_mul(neg_h2[t][:, cols(hf)], banks[t][hf][:], -1.0)
+            else:
+                nc.scalar.activation(neg_h2[t][:, cols(hf)], banks[t][hf][:], ACT.Copy, scale=-1.0)
+            nc.scalar.copy(h2[t][:, cols(hf)], banks[t][hf][:])
+
+        whole = slice(0, S)
+        for hf in range(2):
+            gate(0, cols(hf))
+            complement(0, cols(hf), False)
+            keep(0, cols(hf))
+            mix(0, cols(hf))
+        for t in (1, 2):
+            gate(t, whole)
+            complement(t, whole, True)
+            last_h(t - 1)
+            keep(t, whole)
+            mix(t, whole)
+        gate(3, cols(0))
+        complement(3, cols(0), False)
+        keep(3, cols(0))
+        mix(3, cols(0))
+        gate(3, cols(1))
+        complement(3, cols(1), True)
+        picked = rest[:, 3, cols(0)]
+        nc.scalar.activation(picked, h[3][:].indirect(entries(n1_t, cols(1))), ACT.Copy)
+        second_product(0)
+        keep(3, cols(1))
+        nc.vector.tensor_tensor(mixed[:, 3, cols(1)], picked, rest[:, 3, cols(1)], ALU.mult)
         for t in range(PACK):
-            for hf in range(2):
-                nc.vector.tensor_tensor(st[t][:, cols(hf)], neg_h2[t][:].indirect(entries(n3_t, hf)), h2[t][:, cols(hf)], ALU.add)
+            empty_h2(t, 0)
+        second_product(1)
+        for t in range(PACK):
+            empty_h2(t, 1)
+
+        y = tile("y", [P, 2, PACK, HALF], F32)
+        sg2 = tile("sg2", [P, PACK, S], F32)
+        out_rows = out_0.rearrange("(p t) (f j) -> p f t j", t=PACK, f=2)
         y_plane = tile("y_plane", [P, S], U8)
         words_out = out_1[0].rearrange("p n t -> p (n t)").bitcast(I32)
-        for t in range(PACK):
-            for hf in range(2):
-                sg2 = tile("sg2_%d%d" % (t, hf), [P, HALF], F32)
-                nc.scalar.activation(
-                    sg2[:], st[t][:].indirect(entries(n4_t, hf)), ACT.Sigmoid,
-                    bias=bias2[:, t : t + 1], scale=sl2_t[:, t : t + 1],
-                )
-                nc.vector.tensor_tensor(y[hf][:, t, :], h2[t][:, cols(hf)], sg2[:], ALU.mult)
-                nc.sync.dma_start(out_rows[:, t, cols(hf)], y[hf][:, t, :])
+
+        def difference(t, c):
+            nc.vector.tensor_tensor(st[t][:, c], neg_h2[t][:].indirect(entries(n3_t, c)), h2[t][:, c], ALU.add)
+
+        def gate2(t, c):
+            nc.scalar.activation(
+                sg2[:, t, c], st[t][:].indirect(entries(n4_t, c)), ACT.Sigmoid,
+                bias=bias2[:, t : t + 1], scale=sl2_t[:, t : t + 1],
+            )
+
+        def halves(ap):
+            return ap.rearrange("p (f j) -> p f j", f=2)
+
+        difference(0, cols(0))
+        difference(0, cols(1))
+        for t in range(1, PACK):
+            difference(t, whole)
+        for t in range(PACK - 1):
+            gate2(t, whole)
+            nc.vector.tensor_tensor(y[:, :, t, :], halves(h2[t][:]), halves(sg2[:, t, :]), ALU.mult)
+            nc.sync.dma_start(out_rows[:, :, t, :], y[:, :, t, :])
         for hf in range(2):
+            gate2(3, cols(hf))
+            nc.vector.tensor_tensor(y[:, hf, 3, :], h2[3][:, cols(hf)], sg2[:, 3, cols(hf)], ALU.mult)
+            nc.sync.dma_start(out_rows[:, hf, 3, :], y[:, hf, 3, :])
             y_bf = tile("y_bf%d" % hf, [P, HALF, PACK], BF16)
             y_words = tile("y_words%d" % hf, [P, HALF], U32)
-            nc.vector.tensor_copy(woven(y_bf), planar(y[hf]))
+            nc.vector.tensor_copy(woven(y_bf[:]), planar(y[:, hf]))
             nc.vector.quantize_mx(out=y_words[:].bitcast(FP8X4), scales=y_plane[:, cols(hf)], in_=y_bf[:].rearrange("p c t -> p (c t)"))
             nc.sync.dma_start(words_out[:, cols(hf)], y_words[:].bitcast(I32))
         for q in range(4):

from contextlib import ExitStack

import concourse.mybir as mybir

F32 = mybir.dt.float32
BF16 = mybir.dt.bfloat16
I32 = mybir.dt.int32
U32 = mybir.dt.uint32
U16 = mybir.dt.uint16
U8 = mybir.dt.uint8
FP8X4 = mybir.dt.float8_e4m3fn_x4
ACT = mybir.ActivationFunctionType
ALU = mybir.AluOpType

P = 128
PACK = 4
S = 512
TABLE = 2048
HALF = S // 2
LIST_COLS = S // 16
FLOPS = 2 * 2 * 512 * 512 * 512


def tile_picked_hpqeblehq_none_po_kernel(
    tc, x_words, x_scales, d_words, d_scales, sl, th, gn, w1_words, w1_scales, sl2, th2,
    offs, k1, n1, n2, n3, n4, out_0, out_1, out_2,
):
    nc = tc.nc
    with ExitStack() as ctx:
        sb = ctx.enter_context(tc.tile_pool(name="sb", bufs=1))
        ps = ctx.enter_context(tc.psum_pool(name="ps", bufs=1))

        def tile(name, shape, dtype, tag=None):
            return sb.tile(shape, dtype, name=name, tag=tag or name, align_bytes=64)

        def load_list(name, src):
            dst = tile(name, [P, LIST_COLS], U16)
            nc.sync.dma_start(dst[:], src)
            return dst

        def load_words(name, src, width, queue):
            dst = tile(name, [P, width], U32)
            queue.dma_start(dst[:].bitcast(I32), src[0].rearrange("p n t -> p (n t)").bitcast(I32))
            return dst

        def load_rows(name, src, queue):
            dst = tile(name, [P, PACK], F32)
            queue.dma_start(dst[:], src.rearrange("(p t) o -> p (t o)", t=PACK))
            return dst

        def cols(half):
            return slice(half * HALF, (half + 1) * HALF)

        def entries(lst, c):
            return lst[:, c.start // 16 : c.stop // 16]

        def deal_words(t):
            return t[:].rearrange("p (t c i) -> p c t i", t=PACK, i=4)

        def undealt_words(t):
            return t[:].rearrange("p (c i t) -> p c t i", t=PACK, i=4)

        def woven(t):
            return t.rearrange("p (c i) t -> p c t i", i=2)

        def planar(t):
            return t.rearrange("p t (c i) -> p c t i", i=2)

        d_bytes = tile("d_bytes", [P, TABLE], U8)
        x_bytes = tile("x_bytes", [P, TABLE], U8)
        w_bytes = tile("w_bytes", [P, S], U8)
        planes = tile("planes", [P, 3 * S], U8)
        nc.vector.memset(w_bytes[:].bitcast(I32), 0)
        nc.vector.memset(d_bytes[:].bitcast(I32), 0)
        nc.vector.memset(x_bytes[:].bitcast(I32), 0)
        k1_t = load_list("k1_t", k1)
        offs_t = load_list("offs_t", offs)
        d_tab = load_words("d_tab", d_words, TABLE, nc.sync)
        sl_t = load_rows("sl_t", sl, nc.scalar)
        th_t = load_rows("th_t", th, nc.scalar)
        nc.scalar.dma_start(w_bytes[0:P:8, :].bitcast(I32), w1_scales[0].bitcast(I32))
        nc.scalar.dma_start(d_bytes[0:P:8, :].bitcast(I32), d_scales[0].bitcast(I32))
        nc.scalar.dma_start(x_bytes[0:P:8, :].bitcast(I32), x_scales[0].bitcast(I32))
        gn_t = load_rows("gn_t", gn, nc.gpsimd)
        sl2_t = load_rows("sl2_t", sl2, nc.gpsimd)
        th2_t = load_rows("th2_t", th2, nc.gpsimd)
        n2_t = load_list("n2_t", n2)
        n1_t = load_list("n1_t", n1)
        x_tab = load_words("x_tab", x_words, TABLE, nc.sync)
        w_raw = load_words("w_raw", w1_words, S, nc.sync)
        n3_t = load_list("n3_t", n3)
        n4_t = load_list("n4_t", n4)
        warm = tile("warm", [P, 1], F32)
        nc.scalar.activation(warm[:], sl_t[:, 0:1], ACT.Sigmoid)

        def negated(name, src):
            dst = tile(name, [P, PACK], F32)
            nc.gpsimd.tensor_scalar(dst[:], src[:], -1.0, 0.0, ALU.mult, ALU.add)
            return dst

        def sigmoid_bias(name, slope, threshold):
            dst = tile(name, [P, PACK], F32)
            nc.gpsimd.tensor_tensor(dst[:], negated(name + "_neg", slope)[:], threshold[:], ALU.mult)
            return dst

        bias1 = sigmoid_bias("bias1", sl_t, th_t)
        neg_gn = negated("neg_gn", gn_t)
        bias2 = sigmoid_bias("bias2", sl2_t, th2_t)

        def deal_bytes(engine, dst, src):
            engine.tensor_copy(dst.rearrange("p (t m) -> p t m", t=PACK), src.rearrange("p (m t) -> p t m", t=PACK))

        d_bytes_g = tile("d_bytes_g", [P, S], U8)
        x_bytes_g = tile("x_bytes_g", [P, S], U8)
        deal_bytes(nc.vector, planes[:, 2 * S : 3 * S], w_bytes[:])
        nc.vector.tensor_copy(d_bytes_g[:], d_bytes[:].indirect(k1_t[:]))
        nc.vector.tensor_copy(x_bytes_g[:], x_bytes[:].indirect(offs_t[:]))
        deal_bytes(nc.vector, planes[:, 0:S], d_bytes_g[:])
        nc.vector.tensor_copy(planes[:, S : 2 * S].bitcast(I32), x_bytes_g[:].bitcast(I32))
        for q in range(4):
            nc.scalar.dma_start(planes[32 * q + 4 : 32 * q + 8, :].bitcast(I32), planes[32 * q : 32 * q + 32 : 8, :].bitcast(I32))

        d_g = tile("d_g", [P, S], U32, tag="x_bytes_g")
        d_dealt = tile("d_dealt", [P, S], U32)
        nc.vector.tensor_copy(d_g[:], d_tab[:].indirect(k1_t[:]))
        nc.vector.tensor_copy(deal_words(d_dealt).bitcast(I32), undealt_words(d_g).bitcast(I32))

        w_dealt = tile("w_dealt", [P, S], U32)
        nc.gpsimd.tensor_copy(w_dealt[:].rearrange("p (t m) -> p t m", t=PACK), w_raw[:].rearrange("p (m t) -> p t m", t=PACK))

        h = [tile("h%d" % t, [P, S if t == 0 else 2 * S], F32) for t in range(PACK)]
        st = [tile("st%d" % t, [P, S if t == 3 else 2 * S], F32) for t in range(PACK)]
        for t in range(1, PACK):
            nc.vector.memset(h[t][:, S:], 0.0)
            nc.scalar.copy(st[t - 1][:, S:], h[t][:, S:])

        banks = [[ps.tile([P, HALF], F32, name="bank%d%d" % (t, hf)) for hf in range(2)] for t in range(PACK)]
        x_g = [tile("x_g%d" % hf, [P, HALF], U32) for hf in range(2)]
        for hf in range(2):
            nc.vector.tensor_copy(x_g[hf][:], x_tab[:].indirect(entries(offs_t, cols(hf))))

        def h_bank(t, hf):
            return banks[t][hf] if t < 3 else banks[hf][1]

        def multiply_h(t, hf):
            m = slice(t * P, (t + 1) * P)
            nc.tensor.matmul_mx(
                out=h_bank(t, hf)[:], lhsT=d_dealt[:, m].bitcast(FP8X4), lhsT_scale=planes[4:, m],
                rhs=x_g[hf][:].bitcast(FP8X4), rhs_scale=planes[4:, S + hf * HALF : S + (hf + 1) * HALF],
                start=True, stop=True,
            )

        for t, hf in ((0, 0), (1, 0), (0, 1), (1, 1), (2, 0), (2, 1)):
            multiply_h(t, hf)
            if hf == 0 and t < 2:
                nc.scalar.activation(h[t][:, cols(hf)], h_bank(t, hf)[:], ACT.Copy, scale=0.0625)
            else:
                nc.vector.tensor_scalar_mul(h[t][:, cols(hf)], h_bank(t, hf)[:], 0.0625)

        def last_h(hf):
            multiply_h(3, hf)
            nc.scalar.activation(h[3][:, cols(hf)], h_bank(3, hf)[:], ACT.Copy, scale=0.0625)

        sg = tile("sg", [P, PACK, S], F32)
        rest = tile("rest", [P, PACK, S], F32)
        kept = tile("kept", [P, PACK, S], F32)
        mixed = tile("mixed", [P, PACK, S], F32)
        h2 = [tile("h2_%d" % t, [P, S], F32) for t in range(PACK)]
        neg_h2 = h

        def gate(t, c):
            nc.scalar.activation(
                sg[:, t, c], h[t][:].indirect(entries(n2_t, c)), ACT.Sigmoid,
                bias=bias1[:, t : t + 1], scale=sl_t[:, t : t + 1],
            )

        def complement(t, c, on_scalar):
            if on_scalar:
                nc.scalar.activation(rest[:, t, c], sg[:, t, c], ACT.Identity, bias=gn_t[:, t : t + 1], scale=neg_gn[:, t : t + 1])
            else:
                nc.vector.tensor_scalar(rest[:, t, c], sg[:, t, c], neg_gn[:, t : t + 1], gn_t[:, t : t + 1], ALU.mult, ALU.add)

        def keep(t, c):
            nc.vector.scalar_tensor_tensor(kept[:, t, c], sg[:, t, c], gn_t[:, t : t + 1], h[t][:, c], ALU.mult, ALU.mult)

        def mix(t, c):
            nc.vector.tensor_tensor(mixed[:, t, c], h[t][:].indirect(entries(n1_t, c)), rest[:, t, c], ALU.mult)

        def second_product(hf):
            z = tile("z%d" % hf, [P, HALF, PACK], BF16)
            z_words = tile("z_words%d" % hf, [P, HALF], U32)
            z_plane = tile("z_plane%d" % hf, [P, HALF], U8)
            nc.vector.tensor_tensor(woven(z[:]), planar(kept[:, :, cols(hf)]), planar(mixed[:, :, cols(hf)]), ALU.add)
            nc.vector.quantize_mx(out=z_words[:].bitcast(FP8X4), scales=z_plane[:], in_=z[:].rearrange("p c t -> p (c t)"))
            for t in range(PACK):
                nc.tensor.matmul_mx(
                    out=banks[t][hf][:], lhsT=w_dealt[:, t * P : (t + 1) * P].bitcast(FP8X4),
                    lhsT_scale=planes[4:, 2 * S + t * P : 2 * S + (t + 1) * P],
                    rhs=z_words[:].bitcast(FP8X4), rhs_scale=z_plane[:], start=True, stop=True,
                )

        def empty_h2(t, hf):
            if hf == 1 and t == 0:
                nc.vector.tensor_scalar_mul(neg_h2[t][:, cols(hf)], banks[t][hf][:], -1.0)
            else:
                nc.scalar.activation(neg_h2[t][:, cols(hf)], banks[t][hf][:], ACT.Copy, scale=-1.0)
            nc.scalar.copy(h2[t][:, cols(hf)], banks[t][hf][:])

        whole = slice(0, S)
        for hf in range(2):
            gate(0, cols(hf))
            complement(0, cols(hf), False)
            keep(0, cols(hf))
            mix(0, cols(hf))
        for t in (1, 2):
            gate(t, whole)
            complement(t, whole, True)
            last_h(t - 1)
            keep(t, whole)
            mix(t, whole)
        gate(3, cols(0))
        complement(3, cols(0), False)
        keep(3, cols(0))
        mix(3, cols(0))
        gate(3, cols(1))
        complement(3, cols(1), True)
        picked = rest[:, 3, cols(0)]
        nc.scalar.activation(picked, h[3][:].indirect(entries(n1_t, cols(1))), ACT.Copy)
        second_product(0)
        keep(3, cols(1))
        nc.vector.tensor_tensor(mixed[:, 3, cols(1)], picked, rest[:, 3, cols(1)], ALU.mult)
        for t in range(PACK):
            empty_h2(t, 0)
        second_product(1)
        for t in range(PACK):
            empty_h2(t, 1)

        y = tile("y", [P, 2, PACK, HALF], F32)
        sg2 = tile("sg2", [P, PACK, S], F32)
        out_rows = out_0.rearrange("(p t) (f j) -> p f t j", t=PACK, f=2)
        y_plane = tile("y_plane", [P, S], U8)
        words_out = out_1[0].rearrange("p n t -> p (n t)").bitcast(I32)

        def difference(t, c):
            nc.vector.tensor_tensor(st[t][:, c], neg_h2[t][:].indirect(entries(n3_t, c)), h2[t][:, c], ALU.add)

        def gate2(t, c):
            nc.scalar.activation(
                sg2[:, t, c], st[t][:].indirect(entries(n4_t, c)), ACT.Sigmoid,
                bias=bias2[:, t : t + 1], scale=sl2_t[:, t : t + 1],
            )

        def halves(ap):
            return ap.rearrange("p (f j) -> p f j", f=2)

        difference(0, cols(0))
        difference(0, cols(1))
        for t in range(1, PACK):
            difference(t, whole)
        for t in range(PACK - 1):
            gate2(t, whole)
            nc.vector.tensor_tensor(y[:, :, t, :], halves(h2[t][:]), halves(sg2[:, t, :]), ALU.mult)
            nc.sync.dma_start(out_rows[:, :, t, :], y[:, :, t, :])
        for hf in range(2):
            gate2(3, cols(hf))
            nc.vector.tensor_tensor(y[:, hf, 3, :], h2[3][:, cols(hf)], sg2[:, 3, cols(hf)], ALU.mult)
            nc.sync.dma_start(out_rows[:, hf, 3, :], y[:, hf, 3, :])
            y_bf = tile("y_bf%d" % hf, [P, HALF, PACK], BF16)
            y_words = tile("y_words%d" % hf, [P, HALF], U32)
            nc.vector.tensor_copy(woven(y_bf[:]), planar(y[:, hf]))
            nc.vector.quantize_mx(out=y_words[:].bitcast(FP8X4), scales=y_plane[:, cols(hf)], in_=y_bf[:].rearrange("p c t -> p (c t)"))
            nc.sync.dma_start(words_out[:, cols(hf)], y_words[:].bitcast(I32))
        for q in range(4):
            queue = nc.scalar if q % 2 == 0 else nc.sync
            queue.dma_start(out_2[0][4 * q : 4 * q + 4, :].bitcast(I32), y_plane[32 * q : 32 * q + 4, :].bitcast(I32))
